import numpy as np
CORES = [78,86,94,102,110,118]
N = 6
TK = 512
D = 128 * N
EPS = 0.01
def setup_inputs(rng):
    return {"x": (rng.standard_normal((N, 128, TK), dtype=np.float32) * (0.5 + np.abs(rng.standard_normal((1, 1, TK), dtype=np.float32))) + rng.standard_normal((1, 1, TK), dtype=np.float32)), "w": (rng.standard_normal((N, 128, 128), dtype=np.float32) / 11)}
def reference(x, w):
    X = x.astype(np.float64)
    mu = X.sum(axis=(0, 1)) / D
    Z = X - mu
    Z = Z / np.sqrt((Z ** 2).sum(axis=(0, 1)) / D + EPS)
    s = sum(w[r].astype(np.float64).T @ Z[r] for r in range(N)).astype(np.float32)
    return {"y": np.broadcast_to(s, (N,) + s.shape)}

from concourse.bass import DstId, RemoteDMATransfer
from concourse.mybir import AluOpType, ActivationFunctionType

N = 6
TK = 512
D = 128 * N
EPS = 0.01
W = 88
START = [0, 88, 172, 256, 344, 428]
END = START[1:] + [TK]
SW = 12

SCRATCH = {
    "xs": ("sbuf", [128, TK], "float32"),
    "xq": ("sbuf", [128, TK], "float32"),
    "ws": ("sbuf", [128, 128], "float32"),
    "ones": ("sbuf", [128, 128], "float32"),
    "ident": ("sbuf", [128, 128], "float32"),
    "st": ("sbuf", [128, N * SW], "float32"),
    "sa": ("sbuf", [128, 3 * SW], "float32"),
    "sb": ("sbuf", [128, SW], "float32"),
    "tot": ("sbuf", [128, SW], "float32"),
    "nmu": ("sbuf", [128, 4], "float32"),
    "m2": ("sbuf", [128, 4], "float32"),
    "e2": ("sbuf", [128, 4], "float32"),
    "var": ("sbuf", [128, 4], "float32"),
    "iv": ("sbuf", [128, 4], "float32"),
    "rr": ("sbuf", [128, 4], "float32"),
    "dm": ("sbuf", [128, W], "float32"),
    "dr": ("sbuf", [128, W], "float32"),
    "cm": ("sbuf", [128, W], "float32"),
    "rs": ("sbuf", [128, W], "float32"),
    "ps": ("sbuf", [128, (N - 1) * W], "float32"),
    "rl": ("sbuf", [128, N * W], "float32"),
    "yf": ("sbuf", [128, TK], "float32"),
    "p_st": ("psum", [128, 512], "float32"),
    "p_b": ("psum", [128, 512], "float32"),
    "p_a1": ("psum", [128, 512], "float32"),
    "p_a2": ("psum", [128, 512], "float32"),
    "p_own": ("psum", [128, 512], "float32"),
    "p_m": ("psum", [128, 512], "float32"),
    "p_r": ("psum", [128, 512], "float32"),
}
SEMAPHORES = (["lx0", "lx1", "lx2", "lx3", "lw", "c_ones", "c_id", "sq0", "sq1", "sq2", "sq3", "pe_st", "st_own",
               "st_arr", "pe_b", "pe_a1", "pe_a2", "pe_own", "cp_b", "cp_a1", "cp_a2", "y_own", "sent", "stored"]
              + ["rs%d" % r for r in range(N)] + ["ag%d" % r for r in range(N)] + ["v%d" % i for i in range(32)])


def rank_program(g, core, T, topo):
    me = T.rank_of(core)
    if me is None:
        return
    S = T.sem
    V, PE, ACT, SP = g.vector, g.tensor, g.scalar, g.sync
    add, mult, sub = AluOpType.add, AluOpType.mult, AluOpType.subtract
    F = ActivationFunctionType
    cores = T.cores

    def others(r):
        return [(r + k) % N for k in range(1, N)]

    def engines(r):
        m = -1
        for d in others(r):
            if not topo.may_write(cores[r], cores[d]):
                raise ValueError("rank %d may not write to rank %d" % (r, d))
            m &= topo.mask(cores[r], cores[d])
        return [e for e in range(m.bit_length()) if (m >> e) & 1]

    def bits(es):
        return sum(1 << e for e in es)

    def dst_id(r):
        rid, pid, _se = topo.addr(cores[r])
        return DstId(rid=rid, pnc=pid)

    n_ev = [0]

    def ev():
        n_ev[0] += 1
        return S["v%d" % (n_ev[0] - 1)]

    eng = engines(me)
    n_all = len(eng)
    n_q = n_all // 4
    dests = others(me)
    s0, e0 = START[me], END[me]
    wd = e0 - s0

    def send_from(j):
        return min(START[j], TK - W)

    off = s0 - send_from(me)

    def blk(b):
        return slice(128 * b, 128 * b + 128)
    SP.dma_start(T.xs[:, blk(0)], T.x[:, blk(0)]).then_inc(S.lx0, 16)
    ACT.dma_start(T.xs[:, blk(1)], T.x[:, blk(1)]).then_inc(S.lx1, 16)
    SP.dma_start(T.ws[:], T.w[:]).then_inc(S.lw, 16)
    ACT.dma_start(T.xs[:, blk(2)], T.x[:, blk(2)]).then_inc(S.lx2, 16)
    SP.dma_start(T.xs[:, blk(3)], T.x[:, blk(3)]).then_inc(S.lx3, 16)

    V.memset(T.ones[:], 1.0).then_inc(S.c_ones, 1)
    g.wait_ge(S.c_ones, 1)
    g.affine_select(T.ident[:], T.ones[:], [[-1, 128]], AluOpType.is_equal, 0.0, 0, 1).then_inc(S.c_id, 1)

    for b in range(4):
        ACT.wait_ge(S["lx%d" % b], 16)
        ACT.activation(T.xq[:, blk(b)], T.xs[:, blk(b)], F.Square).then_inc(S["sq%d" % b], 1)
    PE.wait_ge(S.c_ones, 1)
    for b in range(4):
        PE.wait_ge(S["lx%d" % b], 16)
        PE.matmul(T.p_st[:, b:b + 1], T.xs[:, blk(b)], T.ones[:, 0:1], True, True).then_inc(S.pe_st, 1)
        PE.wait_ge(S["sq%d" % b], 1)
        PE.matmul(T.p_st[:, 4 + b:5 + b], T.xq[:, blk(b)], T.ones[:, 0:1], True, True).then_inc(S.pe_st, 1)
    PE.wait_ge(S.lw, 16)
    PE.matmul(T.p_st[:, 8:12], T.ws[:], T.ones[:, 0:4], True, True).then_inc(S.pe_st, 1)
    my_st = T.st[:, SW * me:SW * me + SW]
    V.wait_ge(S.pe_st, 9)
    V.tensor_copy(my_st, T.p_st[:, 0:SW]).then_inc(S.st_own, 1)
    g.wait_ge(S.st_own, 1)
    g.remote_dma_fused([RemoteDMATransfer(dst_ids=[dst_id(d) for d in dests], dma_engine_mask=bits(eng),
                                          remote_sem=S.st_arr, srcs=[my_st], dsts=[my_st for d in dests], alu_op=0)],
                       local_sem=S.sent)

    def p_block(out, j, sem):
        a = send_from(j)
        PE.matmul(out, T.ws[:], T.xs[:, a:a + W], True, True).then_inc(sem, 1)
    p_block(T.p_b[:, 0:W], dests[0], S.pe_b)
    p_block(T.p_a1[:, 0:W], dests[1], S.pe_a1)
    p_block(T.p_a1[:, W:2 * W], dests[2], S.pe_a1)
    p_block(T.p_a2[:, 0:W], dests[3], S.pe_a2)
    p_block(T.p_a2[:, W:2 * W], dests[4], S.pe_a2)
    acc = T.p_own[:, 0:wd]
    PE.matmul(acc, T.ws[:], T.xs[:, s0:e0], True, True).then_inc(S.pe_own, 1)

    V.wait_ge(S.pe_b, 1)
    V.tensor_copy(T.ps[:, 0:W], T.p_b[:, 0:W]).then_inc(S.cp_b, 1)
    V.wait_ge(S.pe_a1, 2)
    V.tensor_copy(T.ps[:, W:3 * W], T.p_a1[:, 0:2 * W]).then_inc(S.cp_a1, 1)
    ACT.wait_ge(S.pe_a2, 2)
    ACT.activation(T.ps[:, 3 * W:5 * W], T.p_a2[:, 0:2 * W], F.Copy).then_inc(S.cp_a2, 1)

    land = T.rl[:, W * me:W * me + W]
    g.wait_ge(S.cp_b, 1)
    g.remote_dma_fused([RemoteDMATransfer(dst_ids=[dst_id(dests[0])], dma_engine_mask=bits(eng),
                                          remote_sem=S["rs%d" % me], srcs=[T.ps[:, 0:W]], dsts=[land], alu_op=0)],
                       local_sem=S.sent)
    g.wait_ge(S.cp_a1, 1)
    g.wait_ge(S.cp_a2, 1)
    g.remote_dma_fused([RemoteDMATransfer(dst_ids=[dst_id(dests[k])], dma_engine_mask=bits(eng[n_q * (k - 1):n_q * k]),
                                          remote_sem=S["rs%d" % me], srcs=[T.ps[:, W * k:W * k + W]], dsts=[land],
                                          alu_op=0) for k in range(1, 5)],
                       local_sem=S.sent)

    V.wait_ge(S.st_own, 1)
    V.wait_ge(S.st_arr, sum(len(engines(r)) for r in dests))
    a1, a2, a3, a4, a5, a6, a7, a8 = [ev() for i in range(8)]
    V.tensor_tensor(T.sa[:], T.st[:, 0:3 * SW], T.st[:, 3 * SW:6 * SW], add).then_inc(a1, 1)
    V.wait_ge(a1, 1)
    V.tensor_tensor(T.sb[:], T.sa[:, 0:SW], T.sa[:, SW:2 * SW], add).then_inc(a2, 1)
    V.wait_ge(a2, 1)
    V.tensor_tensor(T.tot[:], T.sb[:], T.sa[:, 2 * SW:3 * SW], add).then_inc(a3, 1)
    V.wait_ge(a3, 1)
    V.tensor_scalar(T.nmu[:], T.tot[:, 0:4], -1.0 / D, None, mult).then_inc(a4, 1)
    V.tensor_scalar(T.e2[:], T.tot[:, 4:8], 1.0 / D, EPS, mult, add).then_inc(a5, 1)
    V.wait_ge(a4, 1)
    V.tensor_tensor(T.m2[:], T.nmu[:], T.nmu[:], mult).then_inc(a6, 1)
    V.wait_ge(a5, 1)
    V.wait_ge(a6, 1)
    V.tensor_tensor(T.var[:], T.e2[:], T.m2[:], sub).then_inc(a7, 1)
    V.wait_ge(a7, 1)
    V.reciprocal(T.iv[:], T.var[:]).then_inc(a8, 1)

    pieces = [(b, max(s0, 128 * b), min(e0, 128 * b + 128)) for b in range(4) if max(s0, 128 * b) < min(e0, 128 * b + 128)]

    r1, r2, r3, r4 = [ev() for i in range(4)]
    ACT.wait_ge(a8, 1)
    ACT.activation(T.rr[:], T.iv[:], F.Sqrt).then_inc(r1, 1)
    ACT.wait_ge(r1, 1)
    ACT.wait_ge(S.c_id, 1)
    for (b, lo, hi) in pieces:
        ACT.activation(T.dr[:, lo - s0:hi - s0], T.ident[:, lo - 128 * b:hi - 128 * b], F.Identity,
                       scale=T.rr[:, b:b + 1]).then_inc(r2, 1)

    m1, m2, m3, m4 = [ev() for i in range(4)]
    V.wait_ge(S.c_id, 1)
    for (b, lo, hi) in pieces:
        V.tensor_scalar(T.dm[:, lo - s0:hi - s0], T.ident[:, lo - 128 * b:hi - 128 * b], T.nmu[:, b:b + 1], None,
                        mult).then_inc(m1, 1)
    PE.wait_ge(m1, len(pieces))
    PE.matmul(T.p_m[:, 0:wd], T.ones[:], T.dm[:, 0:wd], True, True).then_inc(m2, 1)
    PE.wait_ge(r2, len(pieces))
    PE.matmul(T.p_r[:, 0:wd], T.ones[:], T.dr[:, 0:wd], True, True).then_inc(r3, 1)
    ACT.wait_ge(r3, 1)
    ACT.activation(T.rs[:, 0:wd], T.p_r[:, 0:wd], F.Copy).then_inc(r4, 1)
    V.wait_ge(m2, 1)
    V.tensor_scalar(T.cm[:, 0:wd], T.p_m[:, 0:wd], T.tot[:, 8:9], None, mult).then_inc(m3, 1)
    V.wait_ge(m3, 1)
    V.wait_ge(S.pe_own, 1)
    V.tensor_tensor(acc, acc, T.cm[:, 0:wd], add).then_inc(m4, 1)

    prev = m4
    for k in range(1, N):
        r = (me - k) % N
        V.wait_ge(S["rs%d" % r], len(engines(r)) if k == 1 else len(engines(r)) // 4)
        V.wait_ge(prev, 1)
        nxt = ev()
        V.tensor_tensor(acc, acc, T.rl[:, W * r + off:W * r + off + wd], add).then_inc(nxt, 1)
        prev = nxt
    V.wait_ge(prev, 1)
    V.wait_ge(r4, 1)
    mine = T.yf[:, s0:e0]
    V.tensor_tensor(mine, acc, T.rs[:, 0:wd], mult).then_inc(S.y_own, 1)

    g.wait_ge(S.y_own, 1)
    g.remote_dma_fused([RemoteDMATransfer(dst_ids=[dst_id(d) for d in dests], dma_engine_mask=bits(eng),
                                          remote_sem=S["ag%d" % me], srcs=[mine], dsts=[mine for d in dests], alu_op=0)],
                       local_sem=S.sent)
    n_sent = 3 * n_all + 4 * n_q
    for k in range(1, N):
        r = (me - k) % N
        q = ACT if k % 2 == 1 else SP
        q.wait_ge(S["ag%d" % r], len(engines(r)))
        q.dma_start(T.y[:, START[r]:END[r]], T.yf[:, START[r]:END[r]]).then_inc(S.stored, 16)
        if k == 2:
            SP.wait_ge(S.y_own, 1)
            SP.wait_ge(S.sent, n_sent)
            SP.dma_start(T.y[:, s0:e0], mine).then_inc(S.stored, 16)
    g.wait_ge(S.sent, n_sent)
    g.wait_ge(S.stored, 16 * N)
